import numpy as np
import ml_dtypes


def mxq(x, axis, fmt="e4m3"):
    dtype, down = {"e4m3": (ml_dtypes.float8_e4m3fn, 7), "e5m2": (ml_dtypes.float8_e5m2, 14)}[fmt]
    v = np.moveaxis(np.asarray(x, np.float32).astype(ml_dtypes.bfloat16).astype(np.float64), axis, -1)
    blocks = v.reshape(v.shape[:-1] + (-1, 32))
    amax = np.abs(blocks).max(-1, keepdims=True)
    byte = np.maximum(np.where(amax > 0, np.frexp(amax)[1] - 1 + 127, 0) - down, 1)
    scale = np.exp2(byte - 127.0)
    codes = (blocks / scale).astype(np.float32).astype(dtype).astype(np.float64)
    return np.moveaxis((codes * scale).reshape(v.shape), -1, axis)


WIDE = False


def mx_kscale(k):
    if not WIDE:
        return np.ones(k)
    levels = np.array([10, -10, 5, -5, 0])
    if k % 512:
        return np.exp2(np.random.permutation(np.resize(levels, k // 32))).repeat(32)
    a = np.empty((k // 512, 16))
    for p in range(k // 512):
        a[p, :8] = np.random.permutation(np.resize(levels, 8))
        for g in range(8):
            far = levels[np.abs(levels - a[p, g]) >= 10]
            a[p, g + 8] = far[np.random.randint(len(far))]
    return np.exp2(a.ravel()).repeat(32)


def f64(x):
    return np.asarray(x).astype(np.float64)


def striped8(idx):
    return np.asarray(idx).reshape(8, -1, 16).transpose(0, 2, 1).reshape(128, -1).astype(np.uint16)


def unstriped8(offs):
    return offs.reshape(8, 16, -1).transpose(0, 2, 1).reshape(8, -1).astype(np.int64)


def pick8(x, idx, run):
    r = np.arange(len(x))
    return x[r[:, None], idx[r % (8 * run) // run]]


E2M1 = np.array([0.0, 0.5, 1.0, 1.5, 2.0, 3.0, 4.0, 6.0, -0.0, -0.5, -1.0, -1.5, -2.0, -3.0, -4.0, -6.0])


def pack_weight(w, fmt):
    k, n = w.shape
    w = f64(np.asarray(w, np.float32).astype(ml_dtypes.bfloat16)).reshape(k // 32, 32, n)
    amax = np.abs(w).max(1)
    if fmt == "e4m3":
        byte = np.frexp(amax)[1] - 1 + 127 - 7
    else:
        mant, ex = np.frexp(amax / 6.0)
        byte = np.where(mant > 0.5, ex, ex - 1) + 127
    byte = np.clip(np.where(amax > 0, byte, 1), 1, 254)
    scaled = (w * np.exp2(127.0 - byte)[:, None, :]).reshape(k, n).astype(np.float32)
    by_word = np.ascontiguousarray(scaled.reshape(k // 512, 128, 4, n).transpose(0, 1, 3, 2))
    if fmt == "e4m3":
        words = by_word.astype(ml_dtypes.float8_e4m3fn).view(np.uint8)
    else:
        c = by_word.astype(ml_dtypes.float4_e2m1fn).view(np.uint8) & 0xF
        words = (c[..., 0::2] | (c[..., 1::2] << 4)).reshape(k // 512, 128, 2 * n)
    return np.ascontiguousarray(words), np.ascontiguousarray(byte.astype(np.uint8).reshape(k // 512, 16, n))


def unpack_weight(words, scales, fmt):
    g, _, n = scales.shape
    words = np.ascontiguousarray(words).reshape(g, 128, n, -1)
    if fmt == "e4m3":
        vals = words.view(ml_dtypes.float8_e4m3fn).astype(np.float64)
    else:
        nib = np.empty((g, 128, n, 4), np.uint8)
        nib[..., 0::2] = words & 0xF
        nib[..., 1::2] = words >> 4
        vals = E2M1[nib]
    vals = vals * np.repeat(np.exp2(scales.astype(np.float64) - 127.0), 8, axis=1)[..., None]
    return vals.transpose(0, 1, 3, 2).reshape(g * 512, n)


K, T, J, N, L = 512, 1024, 256, 512, 512


def setup_inputs():
    n = np.random.standard_normal
    idx = np.stack([np.random.permutation(T)[:J] for _ in range(8)])
    fk = mx_kscale(K)
    fl = mx_kscale(L)
    xtp = pack_weight(n((K, T)) / fk[:, None], "e4m3")
    wp = pack_weight(n((K, N)) * 1 / np.sqrt(K) * fk[:, None], "e2m1")
    wsp = pack_weight(n((L, N)) * 1 / np.sqrt(L) * fl[:, None], "e4m3")
    return {
        "xt_words": xtp[0],
        "xt_scales": xtp[1],
        "w_words": wp[0],
        "w_scales": wp[1],
        "sx": (n((L, J)) / fl[:, None]).astype(np.float32),
        "ws_words": wsp[0],
        "ws_scales": wsp[1],
        "offs": striped8(idx),
    }


def reference(xt_words, xt_scales, w_words, w_scales, sx, ws_words, ws_scales, offs):
    idx = unstriped8(offs)
    xtu = unpack_weight(xt_words, xt_scales, "e4m3")
    wu = unpack_weight(w_words, w_scales, "e2m1")
    wsu = unpack_weight(ws_words, ws_scales, "e4m3")
    z = wu.T @ xtu
    sxq = mxq(f64(sx), 0, "e4m3")
    p = wsu.T @ sxq
    pt = np.tanh(p)
    pg = np.zeros((N, T))
    pg[np.arange(N)[:, None], idx[np.arange(N) % 512 // 64]] = pt
    y = z + pg
    return y

@@ -1,0 +1,168 @@
+from contextlib import ExitStack
+
+import concourse.mybir as mybir
+
+K, T, J, N, L = 512, 1024, 256, 512, 512
+FLOPS = 2 * K * N * T + 2 * L * N * J
+
+F32 = mybir.dt.float32
+BF16 = mybir.dt.bfloat16
+I32 = mybir.dt.int32
+U16 = mybir.dt.uint16
+U8 = mybir.dt.uint8
+FP8X4 = mybir.dt.float8_e4m3fn_x4
+FP4X4 = mybir.dt.float4_e2m1fn_x4
+ADD = mybir.AluOpType.add
+TANH = mybir.ActivationFunctionType.Tanh
+
+P = 128
+PACK = 4
+SETS = N // P
+RUN = 4
+HALF_J = J // 2
+BANK = 512
+
+
+def load_scale_rows(queues, plane, scales):
+    for q in range(4):
+        queues[q].dma_start(
+            out=plane[32 * q : 32 * q + 4, :].bitcast(I32),
+            in_=scales[0, 4 * q : 4 * q + 4, :].bitcast(I32),
+        )
+
+
+def deal(engine, dst, src, words_per_run):
+    engine.tensor_copy(
+        out=dst.rearrange("p (s g i) -> p s g i", s=SETS, i=words_per_run),
+        in_=src.rearrange("p (g s i) -> p s g i", s=SETS, i=words_per_run),
+    )
+
+
+def tile_list_head_scatter_on_shared_kernel(tc, xt_words, xt_scales, w_words, w_scales, sx, ws_words, ws_scales, offs, out):
+    nc = tc.nc
+    with ExitStack() as ctx:
+        keep = ctx.enter_context(tc.tile_pool(name="keep", bufs=1))
+        psum = ctx.enter_context(tc.psum_pool(name="psum", bufs=1))
+
+        offsets = keep.tile([P, J // 16], U16, name="offsets")
+        ws_raw = keep.tile([P, N], I32, name="ws_raw")
+        ws_sc_raw = keep.tile([P, N], U8, name="ws_sc_raw")
+        w_raw = keep.tile([P, N // 2], I32, name="w_raw")
+        w_sc_raw = keep.tile([P, N], U8, name="w_sc_raw")
+        sx_raw = [keep.tile([P, PACK, HALF_J], F32, name="sx_raw%d" % a) for a in range(2)]
+        xt_codes = keep.tile([P, T], I32, name="xt_codes", align_bytes=64)
+        xt_sc = keep.tile([P, T], U8, name="xt_sc", align_bytes=64)
+        pages = [keep.tile([P, T], F32, name="page%d" % a) for a in range(3)]
+
+        nc.vector.memset(ws_sc_raw[:].bitcast(I32), 0)
+        nc.gpsimd.memset(w_sc_raw[:].bitcast(I32), 0)
+        nc.gpsimd.memset(xt_sc[:].bitcast(I32), 0)
+        for page in pages:
+            nc.vector.memset(page[:], 0.0)
+
+        sx_rows = sx.rearrange("(p r) j -> p r j", r=PACK)
+        xt_flat = xt_words[0].rearrange("p n t -> p (n t)")
+        nc.sync.dma_start(out=ws_raw[:], in_=ws_words[0].rearrange("p n t -> p (n t)").bitcast(I32))
+        load_scale_rows([nc.scalar] * 4, ws_sc_raw, ws_scales)
+        for a in range(2):
+            nc.sync.dma_start(out=sx_raw[a][:], in_=sx_rows[:, :, a * HALF_J : (a + 1) * HALF_J])
+        nc.sync.dma_start(out=w_raw[:], in_=w_words[0].bitcast(I32))
+        nc.sync.dma_start(offsets[:], offs)
+        nc.sync.dma_start(out=xt_codes[:], in_=xt_flat.bitcast(I32))
+        load_scale_rows([nc.gpsimd, nc.gpsimd, nc.sync, nc.sync], w_sc_raw, w_scales)
+        load_scale_rows([nc.sync] * 4, xt_sc, xt_scales)
+
+        ws_codes = keep.tile([P, N], I32, name="ws_codes", align_bytes=64)
+        ws_sc = keep.tile([P, N], U8, name="ws_sc", align_bytes=64)
+        w_codes = keep.tile([P, 2 * N], U8, name="w_codes", align_bytes=64)
+        w_sc = keep.tile([P, N], U8, name="w_sc", align_bytes=64)
+        deal(nc.vector, ws_codes[:], ws_raw[:], RUN)
+        deal(nc.vector, ws_sc[:].bitcast(I32), ws_sc_raw[:].bitcast(I32), RUN // 4)
+        deal(nc.gpsimd, w_codes[:].bitcast(I32), w_raw[:], RUN // 2)
+        deal(nc.gpsimd, w_sc[:].bitcast(I32), w_sc_raw[:].bitcast(I32), RUN // 4)
+
+        sx_codes = keep.tile([P, J], I32, name="sx_codes", align_bytes=64)
+        sx_sc = keep.tile([P, J], U8, name="sx_sc", align_bytes=64)
+        pt = [keep.tile([P, J], F32, name="pt0"), keep.tile([P, 2 * J], F32, name="pt12"), keep.tile([P, J], F32, name="pt3")]
+
+        def slots(acc, s, cols):
+            rows = slice(s * P, (s + 1) * P)
+            nc.tensor.matmul_mx(
+                out=acc, lhsT=ws_codes[:, rows].bitcast(FP8X4), lhsT_scale=ws_sc[:, rows],
+                rhs=sx_codes[:, cols].bitcast(FP8X4), rhs_scale=sx_sc[:, cols], start=True, stop=True,
+            )
+
+        for a in range(2):
+            cols = slice(a * HALF_J, (a + 1) * HALF_J)
+            grouped = keep.tile([P, HALF_J, PACK], BF16, name="grouped%d" % a, align_bytes=64)
+            nc.vector.tensor_copy(
+                out=grouped[:].rearrange("p (c i) r -> p c r i", i=4),
+                in_=sx_raw[a][:].rearrange("p r (c i) -> p c r i", i=4),
+            )
+            nc.vector.quantize_mx(
+                out=sx_codes[:, cols].bitcast(FP8X4), scales=sx_sc[:, cols],
+                in_=grouped[:].rearrange("p j r -> p (j r)"),
+            )
+            acc = psum.tile([P, HALF_J], F32, name="p0_%d" % a, tag="bank%d" % a)
+            slots(acc[:], 0, cols)
+            nc.scalar.activation(out=pt[0][:, cols], in_=acc[:], func=TANH)
+        acc = psum.tile([P, 2 * J], F32, name="p12", tag="bank2")
+        slots(acc[:, 0:J], 1, slice(0, J))
+        slots(acc[:, J : 2 * J], 2, slice(0, J))
+        nc.scalar.activation(out=pt[1][:], in_=acc[:], func=TANH)
+        acc = psum.tile([P, J], F32, name="p3", tag="bank0")
+        slots(acc[:], 3, slice(0, J))
+        nc.scalar.activation(out=pt[2][:], in_=acc[:], func=TANH)
+        slot_values = [pt[0][:], pt[1][:, 0:J], pt[1][:, J : 2 * J], pt[2][:]]
+
+        z_bank = [3, 4, 5, 6, 7, 1, 2, 0]
+        z = []
+        for s in range(SETS):
+            for a in range(2):
+                acc = psum.tile([P, BANK], F32, name="z%d_%d" % (s, a), tag="bank%d" % z_bank[2 * s + a])
+                nc.tensor.matmul_mx(
+                    out=acc[:], lhsT=w_codes[:, 2 * s * P : 2 * (s + 1) * P].bitcast(FP4X4),
+                    lhsT_scale=w_sc[:, s * P : (s + 1) * P],
+                    rhs=xt_codes[:, a * BANK : (a + 1) * BANK].bitcast(FP8X4), rhs_scale=xt_sc[:, a * BANK : (a + 1) * BANK],
+                    start=True, stop=True,
+                )
+                z.append(acc)
+
+        page_of = [pages[0], pages[1], pages[2], pages[1]]
+        out_sets = out.rearrange("(g s i) t -> s g i t", s=SETS, i=RUN)
+
+        def place(s, j0, j1):
+            nc.vector.tensor_copy(
+                out=page_of[s][:].indirect(offsets[:, j0 // 16 : j1 // 16]), in_=slot_values[s][:, j0:j1]
+            )
+
+        def add_on_vector(s, t0, t1):
+            a = t0 // BANK
+            res = keep.tile([P, t1 - t0], F32, name="res%d_%d" % (s, t0))
+            nc.vector.tensor_tensor(
+                out=res[:], in0=z[2 * s + a][:, t0 - a * BANK : t1 - a * BANK], in1=page_of[s][:, t0:t1], op=ADD
+            )
+            nc.sync.dma_start(out=out_sets[s][:, :, t0:t1], in_=res[:])
+
+        def add_on_gpsimd(s, t0, t1):
+            a = t0 // BANK
+            zs = keep.tile([P, t1 - t0], F32, name="zs%d_%d" % (s, t0))
+            nc.scalar.copy(out=zs[:], in_=z[2 * s + a][:, t0 - a * BANK : t1 - a * BANK])
+            res = keep.tile([P, t1 - t0], F32, name="res%d_%d" % (s, t0))
+            nc.gpsimd.tensor_tensor(out=res[:], in0=zs[:], in1=page_of[s][:, t0:t1], op=ADD)
+            nc.sync.dma_start(out=out_sets[s][:, :, t0:t1], in_=res[:])
+
+        place(0, 0, HALF_J)
+        place(0, HALF_J, J)
+        place(1, 0, J)
+        place(2, 0, J)
+        add_on_gpsimd(0, 0, 512)
+        add_on_gpsimd(0, 512, 1024)
+        add_on_gpsimd(1, 0, 512)
+        add_on_vector(1, 512, 1024)
+        place(3, 0, J)
+        add_on_gpsimd(2, 0, 512)
+        add_on_gpsimd(2, 512, 768)
+        add_on_gpsimd(2, 768, 1024)
+        for t0 in range(0, T, 256):
+            add_on_vector(3, t0, t0 + 256)

@@ -8,6 +8,7 @@ FLOPS = 2 * K * N * T + 2 * L * N * J
 F32 = mybir.dt.float32
 BF16 = mybir.dt.bfloat16
 I32 = mybir.dt.int32
+U32 = mybir.dt.uint32
 U16 = mybir.dt.uint16
 U8 = mybir.dt.uint8
 FP8X4 = mybir.dt.float8_e4m3fn_x4
@@ -31,10 +32,10 @@ def load_scale_rows(queues, plane, scales):
         )
 
 
-def deal(engine, dst, src, words_per_run):
-    engine.tensor_copy(
-        out=dst.rearrange("p (s g i) -> p s g i", s=SETS, i=words_per_run),
-        in_=src.rearrange("p (g s i) -> p s g i", s=SETS, i=words_per_run),
+def deal(copy, dst, src, words_per_run, sets):
+    copy(
+        out=dst.rearrange("p (s g i) -> p s g i", s=sets.stop - sets.start, i=words_per_run),
+        in_=src.rearrange("p (g s i) -> p s g i", s=SETS, i=words_per_run)[:, sets],
     )
 
 
@@ -49,12 +50,11 @@ def tile_list_head_scatter_on_shared_kernel(tc, xt_words, xt_scales, w_words, w_
         ws_sc_raw = keep.tile([P, N], U8, name="ws_sc_raw")
         w_raw = keep.tile([P, N // 2], I32, name="w_raw")
         w_sc_raw = keep.tile([P, N], U8, name="w_sc_raw")
-        sx_raw = [keep.tile([P, PACK, HALF_J], F32, name="sx_raw%d" % a) for a in range(2)]
+        sx_raw = keep.tile([P, PACK, J], F32, name="sx_raw")
         xt_codes = keep.tile([P, T], I32, name="xt_codes", align_bytes=64)
         xt_sc = keep.tile([P, T], U8, name="xt_sc", align_bytes=64)
-        pages = [keep.tile([P, T], F32, name="page%d" % a) for a in range(3)]
+        pages = [keep.tile([P, T], F32, name="page%d" % a) for a in range(2)]
 
-        nc.vector.memset(ws_sc_raw[:].bitcast(I32), 0)
         nc.gpsimd.memset(w_sc_raw[:].bitcast(I32), 0)
         nc.gpsimd.memset(xt_sc[:].bitcast(I32), 0)
         for page in pages:
@@ -63,32 +63,35 @@ def tile_list_head_scatter_on_shared_kernel(tc, xt_words, xt_scales, w_words, w_
         sx_rows = sx.rearrange("(p r) j -> p r j", r=PACK)
         xt_flat = xt_words[0].rearrange("p n t -> p (n t)")
         nc.sync.dma_start(out=ws_raw[:], in_=ws_words[0].rearrange("p n t -> p (n t)").bitcast(I32))
-        load_scale_rows([nc.scalar] * 4, ws_sc_raw, ws_scales)
-        for a in range(2):
-            nc.sync.dma_start(out=sx_raw[a][:], in_=sx_rows[:, :, a * HALF_J : (a + 1) * HALF_J])
-        nc.sync.dma_start(out=w_raw[:], in_=w_words[0].bitcast(I32))
+        load_scale_rows([nc.sync, nc.sync, nc.scalar, nc.scalar], ws_sc_raw, ws_scales)
+        nc.sync.dma_start(out=sx_raw[:], in_=sx_rows)
         nc.sync.dma_start(offsets[:], offs)
         nc.sync.dma_start(out=xt_codes[:], in_=xt_flat.bitcast(I32))
-        load_scale_rows([nc.gpsimd, nc.gpsimd, nc.sync, nc.sync], w_sc_raw, w_scales)
+        nc.sync.dma_start(out=w_raw[:], in_=w_words[0].bitcast(I32))
         load_scale_rows([nc.sync] * 4, xt_sc, xt_scales)
+        load_scale_rows([nc.gpsimd] * 2 + [nc.sync] * 2, w_sc_raw, w_scales)
 
-        ws_codes = keep.tile([P, N], I32, name="ws_codes", align_bytes=64)
+        ws_first = keep.tile([P, 2 * P], I32, name="ws_first", tag="dealt", align_bytes=64)
+        ws_rest = keep.tile([P, 2 * P], I32, name="ws_rest", tag="dealt_rest", align_bytes=64)
+        ws_codes = [ws_first[:, 0:P], ws_first[:, P : 2 * P], ws_rest[:, 0:P], ws_rest[:, P : 2 * P]]
         ws_sc = keep.tile([P, N], U8, name="ws_sc", align_bytes=64)
-        w_codes = keep.tile([P, 2 * N], U8, name="w_codes", align_bytes=64)
-        w_sc = keep.tile([P, N], U8, name="w_sc", align_bytes=64)
-        deal(nc.vector, ws_codes[:], ws_raw[:], RUN)
-        deal(nc.vector, ws_sc[:].bitcast(I32), ws_sc_raw[:].bitcast(I32), RUN // 4)
-        deal(nc.gpsimd, w_codes[:].bitcast(I32), w_raw[:], RUN // 2)
-        deal(nc.gpsimd, w_sc[:].bitcast(I32), w_sc_raw[:].bitcast(I32), RUN // 4)
+        every_set = slice(0, SETS)
+        nc.vector.memset(ws_sc[:].bitcast(I32), 0)
+        for q in range(4):
+            live = slice(32 * q, 32 * q + 4)
+            deal(nc.vector.tensor_copy, ws_sc[live, :].bitcast(I32), ws_sc_raw[live, :].bitcast(I32), RUN // 4, every_set)
+
+        deal(nc.vector.tensor_copy, ws_first[:], ws_raw[:], RUN, slice(0, 2))
+        deal(nc.vector.tensor_copy, ws_rest[:], ws_raw[:], RUN, slice(2, SETS))
 
         sx_codes = keep.tile([P, J], I32, name="sx_codes", align_bytes=64)
         sx_sc = keep.tile([P, J], U8, name="sx_sc", align_bytes=64)
-        pt = [keep.tile([P, J], F32, name="pt0"), keep.tile([P, 2 * J], F32, name="pt12"), keep.tile([P, J], F32, name="pt3")]
+        pt = keep.tile([P, SETS, J], F32, name="pt")
 
         def slots(acc, s, cols):
             rows = slice(s * P, (s + 1) * P)
             nc.tensor.matmul_mx(
-                out=acc, lhsT=ws_codes[:, rows].bitcast(FP8X4), lhsT_scale=ws_sc[:, rows],
+                out=acc, lhsT=ws_codes[s].bitcast(FP8X4), lhsT_scale=ws_sc[:, rows],
                 rhs=sx_codes[:, cols].bitcast(FP8X4), rhs_scale=sx_sc[:, cols], start=True, stop=True,
             )
 
@@ -97,27 +100,29 @@ def tile_list_head_scatter_on_shared_kernel(tc, xt_words, xt_scales, w_words, w_
             grouped = keep.tile([P, HALF_J, PACK], BF16, name="grouped%d" % a, align_bytes=64)
             nc.vector.tensor_copy(
                 out=grouped[:].rearrange("p (c i) r -> p c r i", i=4),
-                in_=sx_raw[a][:].rearrange("p r (c i) -> p c r i", i=4),
+                in_=sx_raw[:, :, cols].rearrange("p r (c i) -> p c r i", i=4),
             )
             nc.vector.quantize_mx(
                 out=sx_codes[:, cols].bitcast(FP8X4), scales=sx_sc[:, cols],
                 in_=grouped[:].rearrange("p j r -> p (j r)"),
             )
-            acc = psum.tile([P, HALF_J], F32, name="p0_%d" % a, tag="bank%d" % a)
-            slots(acc[:], 0, cols)
-            nc.scalar.activation(out=pt[0][:, cols], in_=acc[:], func=TANH)
-        acc = psum.tile([P, 2 * J], F32, name="p12", tag="bank2")
-        slots(acc[:, 0:J], 1, slice(0, J))
-        slots(acc[:, J : 2 * J], 2, slice(0, J))
-        nc.scalar.activation(out=pt[1][:], in_=acc[:], func=TANH)
-        acc = psum.tile([P, J], F32, name="p3", tag="bank0")
-        slots(acc[:], 3, slice(0, J))
-        nc.scalar.activation(out=pt[2][:], in_=acc[:], func=TANH)
-        slot_values = [pt[0][:], pt[1][:, 0:J], pt[1][:, J : 2 * J], pt[2][:]]
+            for s in range(2):
+                acc = psum.tile([P, HALF_J], F32, name="p%d_%d" % (s, a), tag="bank%d" % (2 * a + s))
+                slots(acc[:], s, cols)
+                nc.scalar.activation(out=pt[:, s, cols], in_=acc[:], func=TANH)
+        w_codes = keep.tile([P, 2 * N], U8, name="w_codes", tag="dealt", align_bytes=64)
+        deal(nc.scalar.copy, w_codes[:].bitcast(U32), w_raw[:].bitcast(U32), RUN // 2, every_set)
+        acc = psum.tile([P, 2, J], F32, name="p23", tag="bank4")
+        for s in range(2):
+            slots(acc[:, s, :], 2 + s, slice(0, J))
+        nc.scalar.activation(out=pt[:, 2:SETS, :], in_=acc[:], func=TANH)
+        w_sc = keep.tile([P, N], U8, name="w_sc", tag="dealt_rest", align_bytes=64)
+        deal(nc.scalar.copy, w_sc[:].bitcast(U32), w_sc_raw[:].bitcast(U32), RUN // 4, every_set)
 
-        z_bank = [3, 4, 5, 6, 7, 1, 2, 0]
-        z = []
-        for s in range(SETS):
+        z_bank = [5, 6, 7, 0, 1, 2, 3, 4]
+        z = {}
+
+        def shared(s):
             for a in range(2):
                 acc = psum.tile([P, BANK], F32, name="z%d_%d" % (s, a), tag="bank%d" % z_bank[2 * s + a])
                 nc.tensor.matmul_mx(
@@ -126,43 +131,31 @@ def tile_list_head_scatter_on_shared_kernel(tc, xt_words, xt_scales, w_words, w_
                     rhs=xt_codes[:, a * BANK : (a + 1) * BANK].bitcast(FP8X4), rhs_scale=xt_sc[:, a * BANK : (a + 1) * BANK],
                     start=True, stop=True,
                 )
-                z.append(acc)
+                z[2 * s + a] = acc
 
-        page_of = [pages[0], pages[1], pages[2], pages[1]]
+        page_of = [pages[0], pages[1], pages[0], pages[1]]
         out_sets = out.rearrange("(g s i) t -> s g i t", s=SETS, i=RUN)
 
         def place(s, j0, j1):
             nc.vector.tensor_copy(
-                out=page_of[s][:].indirect(offsets[:, j0 // 16 : j1 // 16]), in_=slot_values[s][:, j0:j1]
+                out=page_of[s][:].indirect(offsets[:, j0 // 16 : j1 // 16]), in_=pt[:, s, j0:j1]
             )
 
-        def add_on_vector(s, t0, t1):
+        def add_on_vector(s, t0, t1, queue):
             a = t0 // BANK
             res = keep.tile([P, t1 - t0], F32, name="res%d_%d" % (s, t0))
             nc.vector.tensor_tensor(
                 out=res[:], in0=z[2 * s + a][:, t0 - a * BANK : t1 - a * BANK], in1=page_of[s][:, t0:t1], op=ADD
             )
-            nc.sync.dma_start(out=out_sets[s][:, :, t0:t1], in_=res[:])
+            queue.dma_start(out=out_sets[s][:, :, t0:t1], in_=res[:])
 
-        def add_on_gpsimd(s, t0, t1):
-            a = t0 // BANK
-            zs = keep.tile([P, t1 - t0], F32, name="zs%d_%d" % (s, t0))
-            nc.scalar.copy(out=zs[:], in_=z[2 * s + a][:, t0 - a * BANK : t1 - a * BANK])
-            res = keep.tile([P, t1 - t0], F32, name="res%d_%d" % (s, t0))
-            nc.gpsimd.tensor_tensor(out=res[:], in0=zs[:], in1=page_of[s][:, t0:t1], op=ADD)
-            nc.sync.dma_start(out=out_sets[s][:, :, t0:t1], in_=res[:])
-
-        place(0, 0, HALF_J)
-        place(0, HALF_J, J)
-        place(1, 0, J)
-        place(2, 0, J)
-        add_on_gpsimd(0, 0, 512)
-        add_on_gpsimd(0, 512, 1024)
-        add_on_gpsimd(1, 0, 512)
-        add_on_vector(1, 512, 1024)
-        place(3, 0, J)
-        add_on_gpsimd(2, 0, 512)
-        add_on_gpsimd(2, 512, 768)
-        add_on_gpsimd(2, 768, 1024)
-        for t0 in range(0, T, 256):
-            add_on_vector(3, t0, t0 + 256)
+        for j0 in (0, HALF_J):
+            for s in range(2):
+                place(s, j0, j0 + HALF_J)
+        for s in range(SETS):
+            shared(s)
+            if s >= 2:
+                place(s, 0, J)
+            width = 256 if s == SETS - 1 else BANK
+            for t0 in range(0, T, width):
+                add_on_vector(s, t0, t0 + width, nc.sync)

@@ -14,6 +14,7 @@ U8 = mybir.dt.uint8
 FP8X4 = mybir.dt.float8_e4m3fn_x4
 FP4X4 = mybir.dt.float4_e2m1fn_x4
 ADD = mybir.AluOpType.add
+COPY = mybir.ActivationFunctionType.Copy
 TANH = mybir.ActivationFunctionType.Tanh
 
 P = 128
@@ -53,18 +54,18 @@ def tile_list_head_scatter_on_shared_kernel(tc, xt_words, xt_scales, w_words, w_
         sx_raw = keep.tile([P, PACK, J], F32, name="sx_raw")
         xt_codes = keep.tile([P, T], I32, name="xt_codes", align_bytes=64)
         xt_sc = keep.tile([P, T], U8, name="xt_sc", align_bytes=64)
-        pages = [keep.tile([P, T], F32, name="page%d" % a) for a in range(2)]
+        pages = [keep.tile([P, T], F32, name="page%d" % a) for a in range(3)]
 
         nc.gpsimd.memset(w_sc_raw[:].bitcast(I32), 0)
         nc.gpsimd.memset(xt_sc[:].bitcast(I32), 0)
         for page in pages:
-            nc.vector.memset(page[:], 0.0)
+            nc.vector.memset(page[:].bitcast(I32), 0)
 
         sx_rows = sx.rearrange("(p r) j -> p r j", r=PACK)
         xt_flat = xt_words[0].rearrange("p n t -> p (n t)")
-        nc.sync.dma_start(out=ws_raw[:], in_=ws_words[0].rearrange("p n t -> p (n t)").bitcast(I32))
-        load_scale_rows([nc.sync, nc.sync, nc.scalar, nc.scalar], ws_sc_raw, ws_scales)
         nc.sync.dma_start(out=sx_raw[:], in_=sx_rows)
+        load_scale_rows([nc.sync, nc.sync, nc.scalar, nc.scalar], ws_sc_raw, ws_scales)
+        nc.sync.dma_start(out=ws_raw[:], in_=ws_words[0].rearrange("p n t -> p (n t)").bitcast(I32))
         nc.sync.dma_start(offsets[:], offs)
         nc.sync.dma_start(out=xt_codes[:], in_=xt_flat.bitcast(I32))
         nc.sync.dma_start(out=w_raw[:], in_=w_words[0].bitcast(I32))
@@ -72,7 +73,7 @@ def tile_list_head_scatter_on_shared_kernel(tc, xt_words, xt_scales, w_words, w_
         load_scale_rows([nc.gpsimd] * 2 + [nc.sync] * 2, w_sc_raw, w_scales)
 
         ws_first = keep.tile([P, 2 * P], I32, name="ws_first", tag="dealt", align_bytes=64)
-        ws_rest = keep.tile([P, 2 * P], I32, name="ws_rest", tag="dealt_rest", align_bytes=64)
+        ws_rest = keep.tile([P, 2 * P], I32, name="ws_rest", align_bytes=64)
         ws_codes = [ws_first[:, 0:P], ws_first[:, P : 2 * P], ws_rest[:, 0:P], ws_rest[:, P : 2 * P]]
         ws_sc = keep.tile([P, N], U8, name="ws_sc", align_bytes=64)
         every_set = slice(0, SETS)
@@ -80,9 +81,6 @@ def tile_list_head_scatter_on_shared_kernel(tc, xt_words, xt_scales, w_words, w_
         for q in range(4):
             live = slice(32 * q, 32 * q + 4)
             deal(nc.vector.tensor_copy, ws_sc[live, :].bitcast(I32), ws_sc_raw[live, :].bitcast(I32), RUN // 4, every_set)
-
-        deal(nc.vector.tensor_copy, ws_first[:], ws_raw[:], RUN, slice(0, 2))
-        deal(nc.vector.tensor_copy, ws_rest[:], ws_raw[:], RUN, slice(2, SETS))
 
         sx_codes = keep.tile([P, J], I32, name="sx_codes", align_bytes=64)
         sx_sc = keep.tile([P, J], U8, name="sx_sc", align_bytes=64)
@@ -98,14 +96,22 @@ def tile_list_head_scatter_on_shared_kernel(tc, xt_words, xt_scales, w_words, w_
         for a in range(2):
             cols = slice(a * HALF_J, (a + 1) * HALF_J)
             grouped = keep.tile([P, HALF_J, PACK], BF16, name="grouped%d" % a, align_bytes=64)
-            nc.vector.tensor_copy(
-                out=grouped[:].rearrange("p (c i) r -> p c r i", i=4),
-                in_=sx_raw[:, :, cols].rearrange("p r (c i) -> p c r i", i=4),
-            )
+            rounded = grouped[:].rearrange("p (c i) r -> p c r i", i=4)
+            exact = sx_raw[:, :, cols].rearrange("p r (c i) -> p c r i", i=4)
+            if a == 0:
+                nc.vector.tensor_copy(out=rounded, in_=exact)
+            else:
+                nc.scalar.activation(out=rounded, in_=exact, func=COPY)
             nc.vector.quantize_mx(
                 out=sx_codes[:, cols].bitcast(FP8X4), scales=sx_sc[:, cols],
                 in_=grouped[:].rearrange("p j r -> p (j r)"),
             )
+
+        deal(nc.scalar.copy, ws_first[:].bitcast(U32), ws_raw[:].bitcast(U32), RUN, slice(0, 2))
+        deal(nc.vector.tensor_copy, ws_rest[:], ws_raw[:], RUN, slice(2, SETS))
+
+        for a in range(2):
+            cols = slice(a * HALF_J, (a + 1) * HALF_J)
             for s in range(2):
                 acc = psum.tile([P, HALF_J], F32, name="p%d_%d" % (s, a), tag="bank%d" % (2 * a + s))
                 slots(acc[:], s, cols)
@@ -116,24 +122,20 @@ def tile_list_head_scatter_on_shared_kernel(tc, xt_words, xt_scales, w_words, w_
         for s in range(2):
             slots(acc[:, s, :], 2 + s, slice(0, J))
         nc.scalar.activation(out=pt[:, 2:SETS, :], in_=acc[:], func=TANH)
-        w_sc = keep.tile([P, N], U8, name="w_sc", tag="dealt_rest", align_bytes=64)
-        deal(nc.scalar.copy, w_sc[:].bitcast(U32), w_sc_raw[:].bitcast(U32), RUN // 4, every_set)
+        w_sc = keep.tile([P, N], U8, name="w_sc", align_bytes=64)
+        deal(nc.gpsimd.tensor_copy, w_sc[:].bitcast(I32), w_sc_raw[:].bitcast(I32), RUN // 4, every_set)
 
-        z_bank = [5, 6, 7, 0, 1, 2, 3, 4]
-        z = {}
+        def shared(s, t0, t1, bank):
+            acc = psum.tile([P, t1 - t0], F32, name="z%d_%d" % (s, t0), tag="bank%d" % bank)
+            nc.tensor.matmul_mx(
+                out=acc[:], lhsT=w_codes[:, 2 * s * P : 2 * (s + 1) * P].bitcast(FP4X4),
+                lhsT_scale=w_sc[:, s * P : (s + 1) * P],
+                rhs=xt_codes[:, t0:t1].bitcast(FP8X4), rhs_scale=xt_sc[:, t0:t1],
+                start=True, stop=True,
+            )
+            return acc
 
-        def shared(s):
-            for a in range(2):
-                acc = psum.tile([P, BANK], F32, name="z%d_%d" % (s, a), tag="bank%d" % z_bank[2 * s + a])
-                nc.tensor.matmul_mx(
-                    out=acc[:], lhsT=w_codes[:, 2 * s * P : 2 * (s + 1) * P].bitcast(FP4X4),
-                    lhsT_scale=w_sc[:, s * P : (s + 1) * P],
-                    rhs=xt_codes[:, a * BANK : (a + 1) * BANK].bitcast(FP8X4), rhs_scale=xt_sc[:, a * BANK : (a + 1) * BANK],
-                    start=True, stop=True,
-                )
-                z[2 * s + a] = acc
-
-        page_of = [pages[0], pages[1], pages[0], pages[1]]
+        page_of = [pages[0], pages[1], pages[2], pages[1]]
         out_sets = out.rearrange("(g s i) t -> s g i t", s=SETS, i=RUN)
 
         def place(s, j0, j1):
@@ -141,21 +143,31 @@ def tile_list_head_scatter_on_shared_kernel(tc, xt_words, xt_scales, w_words, w_
                 out=page_of[s][:].indirect(offsets[:, j0 // 16 : j1 // 16]), in_=pt[:, s, j0:j1]
             )
 
-        def add_on_vector(s, t0, t1, queue):
-            a = t0 // BANK
+        def add_on_vector(s, z, t0, t1):
             res = keep.tile([P, t1 - t0], F32, name="res%d_%d" % (s, t0))
-            nc.vector.tensor_tensor(
-                out=res[:], in0=z[2 * s + a][:, t0 - a * BANK : t1 - a * BANK], in1=page_of[s][:, t0:t1], op=ADD
-            )
-            queue.dma_start(out=out_sets[s][:, :, t0:t1], in_=res[:])
+            nc.vector.tensor_tensor(out=res[:], in0=z, in1=page_of[s][:, t0:t1], op=ADD)
+            nc.sync.dma_start(out=out_sets[s][:, :, t0:t1], in_=res[:])
+
+        def add_on_gpsimd(s, z, t0, t1):
+            zs = keep.tile([P, t1 - t0], F32, name="zs%d_%d" % (s, t0))
+            nc.scalar.copy(out=zs[:], in_=z)
+            res = keep.tile([P, t1 - t0], F32, name="res%d_%d" % (s, t0))
+            nc.gpsimd.tensor_tensor(out=res[:], in0=zs[:], in1=page_of[s][:, t0:t1], op=ADD)
+            nc.scalar.dma_start(out=out_sets[s][:, :, t0:t1], in_=res[:])
 
         for j0 in (0, HALF_J):
             for s in range(2):
                 place(s, j0, j0 + HALF_J)
-        for s in range(SETS):
-            shared(s)
-            if s >= 2:
-                place(s, 0, J)
-            width = 256 if s == SETS - 1 else BANK
-            for t0 in range(0, T, width):
-                add_on_vector(s, t0, t0 + width, nc.sync)
+        place(2, 0, J)
+        add_on_gpsimd(0, shared(0, 0, 512, 5)[:], 0, 512)
+        add_on_gpsimd(0, shared(0, 512, 1024, 6)[:], 512, 1024)
+        add_on_vector(1, shared(1, 0, 512, 7)[:], 0, 512)
+        add_on_vector(1, shared(1, 512, 1024, 0)[:], 512, 1024)
+        place(3, 0, J)
+        add_on_gpsimd(2, shared(2, 0, 512, 1)[:], 0, 512)
+        add_on_gpsimd(2, shared(2, 512, 768, 2)[:], 512, 768)
+        add_on_vector(2, shared(2, 768, 1024, 3)[:], 768, 1024)
+        for a in range(2):
+            z = shared(3, a * BANK, (a + 1) * BANK, 4 + a)
+            for t0 in (0, 256):
+                add_on_vector(3, z[:, t0 : t0 + 256], a * BANK + t0, a * BANK + t0 + 256)

@@ -21,8 +21,13 @@ P = 128
 PACK = 4
 SETS = N // P
 RUN = 4
+LINE = 4
+GROUP = 16
 HALF_J = J // 2
-BANK = 512
+BANKS = 8
+SLOT_BANKS = 5
+HALF_T = T // 2
+QUARTER_T = T // 4
 
 
 def load_scale_rows(queues, plane, scales):
@@ -40,13 +45,15 @@ def deal(copy, dst, src, words_per_run, sets):
     )
 
 
-def tile_list_head_scatter_on_shared_kernel(tc, xt_words, xt_scales, w_words, w_scales, sx, ws_words, ws_scales, offs, out):
+def tile_list_head_scatter_on_shared_kernel(
+    tc, xt_words, xt_scales, w_words, w_scales, sx, ws_words, ws_scales, offs, out
+):
     nc = tc.nc
     with ExitStack() as ctx:
         keep = ctx.enter_context(tc.tile_pool(name="keep", bufs=1))
         psum = ctx.enter_context(tc.psum_pool(name="psum", bufs=1))
 
-        offsets = keep.tile([P, J // 16], U16, name="offsets")
+        offsets = keep.tile([P, J // GROUP], U16, name="offsets")
         ws_raw = keep.tile([P, N], I32, name="ws_raw")
         ws_sc_raw = keep.tile([P, N], U8, name="ws_sc_raw")
         w_raw = keep.tile([P, N // 2], I32, name="w_raw")
@@ -54,23 +61,21 @@ def tile_list_head_scatter_on_shared_kernel(tc, xt_words, xt_scales, w_words, w_
         sx_raw = keep.tile([P, PACK, J], F32, name="sx_raw")
         xt_codes = keep.tile([P, T], I32, name="xt_codes", align_bytes=64)
         xt_sc = keep.tile([P, T], U8, name="xt_sc", align_bytes=64)
-        pages = [keep.tile([P, T], F32, name="page%d" % a) for a in range(3)]
+        pages = [keep.tile([P, T], F32, name="page%d" % i) for i in range(SETS - 1)]
 
         nc.gpsimd.memset(w_sc_raw[:].bitcast(I32), 0)
         nc.gpsimd.memset(xt_sc[:].bitcast(I32), 0)
         for page in pages:
             nc.vector.memset(page[:].bitcast(I32), 0)
 
-        sx_rows = sx.rearrange("(p r) j -> p r j", r=PACK)
-        xt_flat = xt_words[0].rearrange("p n t -> p (n t)")
-        nc.sync.dma_start(out=sx_raw[:], in_=sx_rows)
+        nc.sync.dma_start(out=sx_raw[:], in_=sx.rearrange("(p r) j -> p r j", r=PACK))
         load_scale_rows([nc.sync, nc.sync, nc.scalar, nc.scalar], ws_sc_raw, ws_scales)
-        nc.sync.dma_start(out=ws_raw[:], in_=ws_words[0].rearrange("p n t -> p (n t)").bitcast(I32))
+        nc.sync.dma_start(out=ws_raw[:], in_=ws_words[0].rearrange("p n r -> p (n r)").bitcast(I32))
         nc.sync.dma_start(offsets[:], offs)
-        nc.sync.dma_start(out=xt_codes[:], in_=xt_flat.bitcast(I32))
+        nc.sync.dma_start(out=xt_codes[:], in_=xt_words[0].rearrange("p t r -> p (t r)").bitcast(I32))
         nc.sync.dma_start(out=w_raw[:], in_=w_words[0].bitcast(I32))
+        load_scale_rows([nc.gpsimd, nc.gpsimd, nc.sync, nc.sync], w_sc_raw, w_scales)
         load_scale_rows([nc.sync] * 4, xt_sc, xt_scales)
-        load_scale_rows([nc.gpsimd] * 2 + [nc.sync] * 2, w_sc_raw, w_scales)
 
         ws_first = keep.tile([P, 2 * P], I32, name="ws_first", tag="dealt", align_bytes=64)
         ws_rest = keep.tile([P, 2 * P], I32, name="ws_rest", align_bytes=64)
@@ -86,88 +91,118 @@ def tile_list_head_scatter_on_shared_kernel(tc, xt_words, xt_scales, w_words, w_
         sx_sc = keep.tile([P, J], U8, name="sx_sc", align_bytes=64)
         pt = keep.tile([P, SETS, J], F32, name="pt")
 
-        def slots(acc, s, cols):
-            rows = slice(s * P, (s + 1) * P)
-            nc.tensor.matmul_mx(
-                out=acc, lhsT=ws_codes[s].bitcast(FP8X4), lhsT_scale=ws_sc[:, rows],
-                rhs=sx_codes[:, cols].bitcast(FP8X4), rhs_scale=sx_sc[:, cols], start=True, stop=True,
-            )
-
-        for a in range(2):
-            cols = slice(a * HALF_J, (a + 1) * HALF_J)
-            grouped = keep.tile([P, HALF_J, PACK], BF16, name="grouped%d" % a, align_bytes=64)
-            rounded = grouped[:].rearrange("p (c i) r -> p c r i", i=4)
-            exact = sx_raw[:, :, cols].rearrange("p r (c i) -> p c r i", i=4)
-            if a == 0:
+        for half in range(2):
+            cols = slice(half * HALF_J, (half + 1) * HALF_J)
+            grouped = keep.tile([P, HALF_J, PACK], BF16, name="grouped%d" % half, align_bytes=64)
+            rounded = grouped[:].rearrange("p (c i) r -> p c r i", i=LINE)
+            exact = sx_raw[:, :, cols].rearrange("p r (c i) -> p c r i", i=LINE)
+            if half == 0:
                 nc.vector.tensor_copy(out=rounded, in_=exact)
             else:
                 nc.scalar.activation(out=rounded, in_=exact, func=COPY)
             nc.vector.quantize_mx(
-                out=sx_codes[:, cols].bitcast(FP8X4), scales=sx_sc[:, cols],
+                out=sx_codes[:, cols].bitcast(FP8X4),
+                scales=sx_sc[:, cols],
                 in_=grouped[:].rearrange("p j r -> p (j r)"),
             )
 
         deal(nc.scalar.copy, ws_first[:].bitcast(U32), ws_raw[:].bitcast(U32), RUN, slice(0, 2))
         deal(nc.vector.tensor_copy, ws_rest[:], ws_raw[:], RUN, slice(2, SETS))
 
-        for a in range(2):
-            cols = slice(a * HALF_J, (a + 1) * HALF_J)
+        def slot_product(acc, s, cols):
+            nc.tensor.matmul_mx(
+                out=acc,
+                lhsT=ws_codes[s].bitcast(FP8X4),
+                lhsT_scale=ws_sc[:, s * P : (s + 1) * P],
+                rhs=sx_codes[:, cols].bitcast(FP8X4),
+                rhs_scale=sx_sc[:, cols],
+                start=True,
+                stop=True,
+            )
+
+        for half in range(2):
+            cols = slice(half * HALF_J, (half + 1) * HALF_J)
             for s in range(2):
-                acc = psum.tile([P, HALF_J], F32, name="p%d_%d" % (s, a), tag="bank%d" % (2 * a + s))
-                slots(acc[:], s, cols)
+                acc = psum.tile([P, HALF_J], F32, name="p%d_%d" % (s, half), tag="bank%d" % (2 * half + s))
+                slot_product(acc[:], s, cols)
                 nc.scalar.activation(out=pt[:, s, cols], in_=acc[:], func=TANH)
-        w_codes = keep.tile([P, 2 * N], U8, name="w_codes", tag="dealt", align_bytes=64)
-        deal(nc.scalar.copy, w_codes[:].bitcast(U32), w_raw[:].bitcast(U32), RUN // 2, every_set)
-        acc = psum.tile([P, 2, J], F32, name="p23", tag="bank4")
-        for s in range(2):
-            slots(acc[:, s, :], 2 + s, slice(0, J))
+
+        w_first = keep.tile([P, 2 * P], U8, name="w_first", align_bytes=64)
+        w_rest = keep.tile([P, 2 * (N - P)], U8, name="w_rest", tag="dealt", align_bytes=64)
+        w_codes = [w_first[:]] + [w_rest[:, 2 * P * i : 2 * P * (i + 1)] for i in range(SETS - 1)]
+        deal(nc.gpsimd.tensor_copy, w_first[:].bitcast(I32), w_raw[:], RUN // 2, slice(0, 1))
+        deal(nc.scalar.copy, w_rest[:].bitcast(U32), w_raw[:].bitcast(U32), RUN // 2, slice(1, SETS))
+
+        acc = psum.tile([P, 2, J], F32, name="p23", tag="bank%d" % (SLOT_BANKS - 1))
+        for i in range(2):
+            slot_product(acc[:, i, :], 2 + i, slice(0, J))
         nc.scalar.activation(out=pt[:, 2:SETS, :], in_=acc[:], func=TANH)
+
         w_sc = keep.tile([P, N], U8, name="w_sc", align_bytes=64)
         deal(nc.gpsimd.tensor_copy, w_sc[:].bitcast(I32), w_sc_raw[:].bitcast(I32), RUN // 4, every_set)
 
-        def shared(s, t0, t1, bank):
-            acc = psum.tile([P, t1 - t0], F32, name="z%d_%d" % (s, t0), tag="bank%d" % bank)
-            nc.tensor.matmul_mx(
-                out=acc[:], lhsT=w_codes[:, 2 * s * P : 2 * (s + 1) * P].bitcast(FP4X4),
-                lhsT_scale=w_sc[:, s * P : (s + 1) * P],
-                rhs=xt_codes[:, t0:t1].bitcast(FP8X4), rhs_scale=xt_sc[:, t0:t1],
-                start=True, stop=True,
-            )
-            return acc
-
         page_of = [pages[0], pages[1], pages[2], pages[1]]
         out_sets = out.rearrange("(g s i) t -> s g i t", s=SETS, i=RUN)
+        res = [keep.tile([P, T], F32, name="res%d" % s) for s in range(SETS)]
+        z_tiles = []
 
         def place(s, j0, j1):
             nc.vector.tensor_copy(
-                out=page_of[s][:].indirect(offsets[:, j0 // 16 : j1 // 16]), in_=pt[:, s, j0:j1]
+                out=page_of[s][:].indirect(offsets[:, j0 // GROUP : j1 // GROUP]), in_=pt[:, s, j0:j1]
             )
 
-        def add_on_vector(s, z, t0, t1):
-            res = keep.tile([P, t1 - t0], F32, name="res%d_%d" % (s, t0))
-            nc.vector.tensor_tensor(out=res[:], in0=z, in1=page_of[s][:, t0:t1], op=ADD)
-            nc.sync.dma_start(out=out_sets[s][:, :, t0:t1], in_=res[:])
+        def shared_product(s, t0, t1):
+            bank = (SLOT_BANKS + len(z_tiles)) % BANKS
+            z = psum.tile([P, t1 - t0], F32, name="z%d_%d" % (s, t0), tag="bank%d" % bank)
+            nc.tensor.matmul_mx(
+                out=z[:],
+                lhsT=w_codes[s].bitcast(FP4X4),
+                lhsT_scale=w_sc[:, s * P : (s + 1) * P],
+                rhs=xt_codes[:, t0:t1].bitcast(FP8X4),
+                rhs_scale=xt_sc[:, t0:t1],
+                start=True,
+                stop=True,
+            )
+            z_tiles.append(z)
+            return z
 
-        def add_on_gpsimd(s, z, t0, t1):
-            zs = keep.tile([P, t1 - t0], F32, name="zs%d_%d" % (s, t0))
-            nc.scalar.copy(out=zs[:], in_=z)
-            res = keep.tile([P, t1 - t0], F32, name="res%d_%d" % (s, t0))
-            nc.gpsimd.tensor_tensor(out=res[:], in0=zs[:], in1=page_of[s][:, t0:t1], op=ADD)
-            nc.scalar.dma_start(out=out_sets[s][:, :, t0:t1], in_=res[:])
+        def add_on_vector(s, z, t0, t1):
+            nc.vector.tensor_tensor(out=res[s][:, t0:t1], in0=z, in1=page_of[s][:, t0:t1], op=ADD)
+
+        def add_on_gpsimd(s, t0, t1):
+            z = shared_product(s, t0, t1)
+            z_sb = keep.tile([P, t1 - t0], F32, name="z_sb%d_%d" % (s, t0))
+            nc.scalar.copy(out=z_sb[:], in_=z[:])
+            nc.gpsimd.tensor_tensor(out=res[s][:, t0:t1], in0=z_sb[:], in1=page_of[s][:, t0:t1], op=ADD)
+
+        def store(queue, s, t0, t1):
+            queue.dma_start(out=out_sets[s][:, :, t0:t1], in_=res[s][:, t0:t1])
 
         for j0 in (0, HALF_J):
             for s in range(2):
                 place(s, j0, j0 + HALF_J)
         place(2, 0, J)
-        add_on_gpsimd(0, shared(0, 0, 512, 5)[:], 0, 512)
-        add_on_gpsimd(0, shared(0, 512, 1024, 6)[:], 512, 1024)
-        add_on_vector(1, shared(1, 0, 512, 7)[:], 0, 512)
-        add_on_vector(1, shared(1, 512, 1024, 0)[:], 512, 1024)
+
+        add_on_gpsimd(0, 0, QUARTER_T)
+        add_on_gpsimd(0, QUARTER_T, HALF_T)
+        add_on_gpsimd(0, HALF_T, T)
+        store(nc.scalar, 0, 0, T)
+
+        for t0 in (0, HALF_T):
+            add_on_vector(1, shared_product(1, t0, t0 + HALF_T)[:], t0, t0 + HALF_T)
+        store(nc.sync, 1, 0, T)
         place(3, 0, J)
-        add_on_gpsimd(2, shared(2, 0, 512, 1)[:], 0, 512)
-        add_on_gpsimd(2, shared(2, 512, 768, 2)[:], 512, 768)
-        add_on_vector(2, shared(2, 768, 1024, 3)[:], 768, 1024)
-        for a in range(2):
-            z = shared(3, a * BANK, (a + 1) * BANK, 4 + a)
-            for t0 in (0, 256):
-                add_on_vector(3, z[:, t0 : t0 + 256], a * BANK + t0, a * BANK + t0 + 256)
+
+        last_quarter = T - QUARTER_T
+        for t0, t1 in ((0, HALF_T), (HALF_T, last_quarter)):
+            add_on_gpsimd(2, t0, t1)
+            store(nc.scalar, 2, t0, t1)
+        add_on_vector(2, shared_product(2, last_quarter, T)[:], last_quarter, T)
+        store(nc.sync, 2, last_quarter, T)
+
+        add_on_vector(3, shared_product(3, 0, HALF_T)[:], 0, HALF_T)
+        store(nc.sync, 3, 0, HALF_T)
+        z = shared_product(3, HALF_T, T)
+        for t0 in (HALF_T, last_quarter):
+            add_on_vector(3, z[:, t0 - HALF_T : t0 - HALF_T + QUARTER_T], t0, t0 + QUARTER_T)
+            store(nc.sync, 3, t0, t0 + QUARTER_T)

from contextlib import ExitStack

import concourse.mybir as mybir

K, T, J, N, L = 512, 1024, 256, 512, 512
FLOPS = 2 * K * N * T + 2 * L * N * J

F32 = mybir.dt.float32
BF16 = mybir.dt.bfloat16
I32 = mybir.dt.int32
U32 = mybir.dt.uint32
U16 = mybir.dt.uint16
U8 = mybir.dt.uint8
FP8X4 = mybir.dt.float8_e4m3fn_x4
FP4X4 = mybir.dt.float4_e2m1fn_x4
ADD = mybir.AluOpType.add
COPY = mybir.ActivationFunctionType.Copy
TANH = mybir.ActivationFunctionType.Tanh

P = 128
PACK = 4
SETS = N // P
RUN = 4
LINE = 4
GROUP = 16
HALF_J = J // 2
BANKS = 8
SLOT_BANKS = 5
HALF_T = T // 2
QUARTER_T = T // 4


def load_scale_rows(queues, plane, scales):
    for q in range(4):
        queues[q].dma_start(
            out=plane[32 * q : 32 * q + 4, :].bitcast(I32),
            in_=scales[0, 4 * q : 4 * q + 4, :].bitcast(I32),
        )


def deal(copy, dst, src, words_per_run, sets):
    copy(
        out=dst.rearrange("p (s g i) -> p s g i", s=sets.stop - sets.start, i=words_per_run),
        in_=src.rearrange("p (g s i) -> p s g i", s=SETS, i=words_per_run)[:, sets],
    )


def tile_list_head_scatter_on_shared_kernel(
    tc, xt_words, xt_scales, w_words, w_scales, sx, ws_words, ws_scales, offs, out
):
    nc = tc.nc
    with ExitStack() as ctx:
        keep = ctx.enter_context(tc.tile_pool(name="keep", bufs=1))
        psum = ctx.enter_context(tc.psum_pool(name="psum", bufs=1))

        offsets = keep.tile([P, J // GROUP], U16, name="offsets")
        ws_raw = keep.tile([P, N], I32, name="ws_raw")
        ws_sc_raw = keep.tile([P, N], U8, name="ws_sc_raw")
        w_raw = keep.tile([P, N // 2], I32, name="w_raw")
        w_sc_raw = keep.tile([P, N], U8, name="w_sc_raw")
        sx_raw = keep.tile([P, PACK, J], F32, name="sx_raw")
        xt_codes = keep.tile([P, T], I32, name="xt_codes", align_bytes=64)
        xt_sc = keep.tile([P, T], U8, name="xt_sc", align_bytes=64)
        pages = [keep.tile([P, T], F32, name="page%d" % i) for i in range(SETS - 1)]

        nc.gpsimd.memset(w_sc_raw[:].bitcast(I32), 0)
        nc.gpsimd.memset(xt_sc[:].bitcast(I32), 0)
        for page in pages:
            nc.vector.memset(page[:].bitcast(I32), 0)

        nc.sync.dma_start(out=sx_raw[:], in_=sx.rearrange("(p r) j -> p r j", r=PACK))
        load_scale_rows([nc.sync, nc.sync, nc.scalar, nc.scalar], ws_sc_raw, ws_scales)
        nc.sync.dma_start(out=ws_raw[:], in_=ws_words[0].rearrange("p n r -> p (n r)").bitcast(I32))
        nc.sync.dma_start(offsets[:], offs)
        nc.sync.dma_start(out=xt_codes[:], in_=xt_words[0].rearrange("p t r -> p (t r)").bitcast(I32))
        nc.sync.dma_start(out=w_raw[:], in_=w_words[0].bitcast(I32))
        load_scale_rows([nc.gpsimd, nc.gpsimd, nc.sync, nc.sync], w_sc_raw, w_scales)
        load_scale_rows([nc.sync] * 4, xt_sc, xt_scales)

        ws_first = keep.tile([P, 2 * P], I32, name="ws_first", tag="dealt", align_bytes=64)
        ws_rest = keep.tile([P, 2 * P], I32, name="ws_rest", align_bytes=64)
        ws_codes = [ws_first[:, 0:P], ws_first[:, P : 2 * P], ws_rest[:, 0:P], ws_rest[:, P : 2 * P]]
        ws_sc = keep.tile([P, N], U8, name="ws_sc", align_bytes=64)
        every_set = slice(0, SETS)
        nc.vector.memset(ws_sc[:].bitcast(I32), 0)
        for q in range(4):
            live = slice(32 * q, 32 * q + 4)
            deal(nc.vector.tensor_copy, ws_sc[live, :].bitcast(I32), ws_sc_raw[live, :].bitcast(I32), RUN // 4, every_set)

        sx_codes = keep.tile([P, J], I32, name="sx_codes", align_bytes=64)
        sx_sc = keep.tile([P, J], U8, name="sx_sc", align_bytes=64)
        pt = keep.tile([P, SETS, J], F32, name="pt")

        for half in range(2):
            cols = slice(half * HALF_J, (half + 1) * HALF_J)
            grouped = keep.tile([P, HALF_J, PACK], BF16, name="grouped%d" % half, align_bytes=64)
            rounded = grouped[:].rearrange("p (c i) r -> p c r i", i=LINE)
            exact = sx_raw[:, :, cols].rearrange("p r (c i) -> p c r i", i=LINE)
            if half == 0:
                nc.vector.tensor_copy(out=rounded, in_=exact)
            else:
                nc.scalar.activation(out=rounded, in_=exact, func=COPY)
            nc.vector.quantize_mx(
                out=sx_codes[:, cols].bitcast(FP8X4),
                scales=sx_sc[:, cols],
                in_=grouped[:].rearrange("p j r -> p (j r)"),
            )

        deal(nc.scalar.copy, ws_first[:].bitcast(U32), ws_raw[:].bitcast(U32), RUN, slice(0, 2))
        deal(nc.vector.tensor_copy, ws_rest[:], ws_raw[:], RUN, slice(2, SETS))

        def slot_product(acc, s, cols):
            nc.tensor.matmul_mx(
                out=acc,
                lhsT=ws_codes[s].bitcast(FP8X4),
                lhsT_scale=ws_sc[:, s * P : (s + 1) * P],
                rhs=sx_codes[:, cols].bitcast(FP8X4),
                rhs_scale=sx_sc[:, cols],
                start=True,
                stop=True,
            )

        for half in range(2):
            cols = slice(half * HALF_J, (half + 1) * HALF_J)
            for s in range(2):
                acc = psum.tile([P, HALF_J], F32, name="p%d_%d" % (s, half), tag="bank%d" % (2 * half + s))
                slot_product(acc[:], s, cols)
                nc.scalar.activation(out=pt[:, s, cols], in_=acc[:], func=TANH)

        w_first = keep.tile([P, 2 * P], U8, name="w_first", align_bytes=64)
        w_rest = keep.tile([P, 2 * (N - P)], U8, name="w_rest", tag="dealt", align_bytes=64)
        w_codes = [w_first[:]] + [w_rest[:, 2 * P * i : 2 * P * (i + 1)] for i in range(SETS - 1)]
        deal(nc.gpsimd.tensor_copy, w_first[:].bitcast(I32), w_raw[:], RUN // 2, slice(0, 1))
        deal(nc.scalar.copy, w_rest[:].bitcast(U32), w_raw[:].bitcast(U32), RUN // 2, slice(1, SETS))

        acc = psum.tile([P, 2, J], F32, name="p23", tag="bank%d" % (SLOT_BANKS - 1))
        for i in range(2):
            slot_product(acc[:, i, :], 2 + i, slice(0, J))
        nc.scalar.activation(out=pt[:, 2:SETS, :], in_=acc[:], func=TANH)

        w_sc = keep.tile([P, N], U8, name="w_sc", align_bytes=64)
        deal(nc.gpsimd.tensor_copy, w_sc[:].bitcast(I32), w_sc_raw[:].bitcast(I32), RUN // 4, every_set)

        page_of = [pages[0], pages[1], pages[2], pages[1]]
        out_sets = out.rearrange("(g s i) t -> s g i t", s=SETS, i=RUN)
        res = [keep.tile([P, T], F32, name="res%d" % s) for s in range(SETS)]
        z_tiles = []

        def place(s, j0, j1):
            nc.vector.tensor_copy(
                out=page_of[s][:].indirect(offsets[:, j0 // GROUP : j1 // GROUP]), in_=pt[:, s, j0:j1]
            )

        def shared_product(s, t0, t1):
            bank = (SLOT_BANKS + len(z_tiles)) % BANKS
            z = psum.tile([P, t1 - t0], F32, name="z%d_%d" % (s, t0), tag="bank%d" % bank)
            nc.tensor.matmul_mx(
                out=z[:],
                lhsT=w_codes[s].bitcast(FP4X4),
                lhsT_scale=w_sc[:, s * P : (s + 1) * P],
                rhs=xt_codes[:, t0:t1].bitcast(FP8X4),
                rhs_scale=xt_sc[:, t0:t1],
                start=True,
                stop=True,
            )
            z_tiles.append(z)
            return z

        def add_on_vector(s, z, t0, t1):
            nc.vector.tensor_tensor(out=res[s][:, t0:t1], in0=z, in1=page_of[s][:, t0:t1], op=ADD)

        def add_on_gpsimd(s, t0, t1):
            z = shared_product(s, t0, t1)
            z_sb = keep.tile([P, t1 - t0], F32, name="z_sb%d_%d" % (s, t0))
            nc.scalar.copy(out=z_sb[:], in_=z[:])
            nc.gpsimd.tensor_tensor(out=res[s][:, t0:t1], in0=z_sb[:], in1=page_of[s][:, t0:t1], op=ADD)

        def store(queue, s, t0, t1):
            queue.dma_start(out=out_sets[s][:, :, t0:t1], in_=res[s][:, t0:t1])

        for j0 in (0, HALF_J):
            for s in range(2):
                place(s, j0, j0 + HALF_J)
        place(2, 0, J)

        add_on_gpsimd(0, 0, QUARTER_T)
        add_on_gpsimd(0, QUARTER_T, HALF_T)
        add_on_gpsimd(0, HALF_T, T)
        store(nc.scalar, 0, 0, T)

        for t0 in (0, HALF_T):
            add_on_vector(1, shared_product(1, t0, t0 + HALF_T)[:], t0, t0 + HALF_T)
        store(nc.sync, 1, 0, T)
        place(3, 0, J)

        last_quarter = T - QUARTER_T
        for t0, t1 in ((0, HALF_T), (HALF_T, last_quarter)):
            add_on_gpsimd(2, t0, t1)
            store(nc.scalar, 2, t0, t1)
        add_on_vector(2, shared_product(2, last_quarter, T)[:], last_quarter, T)
        store(nc.sync, 2, last_quarter, T)

        add_on_vector(3, shared_product(3, 0, HALF_T)[:], 0, HALF_T)
        store(nc.sync, 3, 0, HALF_T)
        z = shared_product(3, HALF_T, T)
        for t0 in (HALF_T, last_quarter):
            add_on_vector(3, z[:, t0 - HALF_T : t0 - HALF_T + QUARTER_T], t0, t0 + QUARTER_T)
            store(nc.sync, 3, t0, t0 + QUARTER_T)
